import numpy as np
import ml_dtypes


def mxq(x, axis, fmt="e4m3"):
    dtype, down = {"e4m3": (ml_dtypes.float8_e4m3fn, 7), "e5m2": (ml_dtypes.float8_e5m2, 14)}[fmt]
    v = np.moveaxis(np.asarray(x, np.float32).astype(ml_dtypes.bfloat16).astype(np.float64), axis, -1)
    blocks = v.reshape(v.shape[:-1] + (-1, 32))
    amax = np.abs(blocks).max(-1, keepdims=True)
    byte = np.maximum(np.where(amax > 0, np.frexp(amax)[1] - 1 + 127, 0) - down, 1)
    scale = np.exp2(byte - 127.0)
    codes = (blocks / scale).astype(np.float32).astype(dtype).astype(np.float64)
    return np.moveaxis((codes * scale).reshape(v.shape), -1, axis)


WIDE = False


def mx_kscale(k):
    if not WIDE:
        return np.ones(k)
    levels = np.array([10, -10, 5, -5, 0])
    if k % 512:
        return np.exp2(np.random.permutation(np.resize(levels, k // 32))).repeat(32)
    a = np.empty((k // 512, 16))
    for p in range(k // 512):
        a[p, :8] = np.random.permutation(np.resize(levels, 8))
        for g in range(8):
            far = levels[np.abs(levels - a[p, g]) >= 10]
            a[p, g + 8] = far[np.random.randint(len(far))]
    return np.exp2(a.ravel()).repeat(32)


BF16 = ml_dtypes.bfloat16


def bf(x):
    return np.asarray(x, np.float32).astype(BF16)


def f64(x):
    return np.asarray(x).astype(np.float64)


E2M1 = np.array([0.0, 0.5, 1.0, 1.5, 2.0, 3.0, 4.0, 6.0, -0.0, -0.5, -1.0, -1.5, -2.0, -3.0, -4.0, -6.0])


def pack_weight(w, fmt):
    k, n = w.shape
    w = f64(bf(w)).reshape(k // 32, 32, n)
    amax = np.abs(w).max(1)
    if fmt == "e4m3":
        byte = np.frexp(amax)[1] - 1 + 127 - 7
    else:
        mant, ex = np.frexp(amax / 6.0)
        byte = np.where(mant > 0.5, ex, ex - 1) + 127
    byte = np.clip(np.where(amax > 0, byte, 1), 1, 254)
    scaled = (w * np.exp2(127.0 - byte)[:, None, :]).reshape(k, n).astype(np.float32)
    by_word = np.ascontiguousarray(scaled.reshape(k // 512, 128, 4, n).transpose(0, 1, 3, 2))
    if fmt == "e4m3":
        words = by_word.astype(ml_dtypes.float8_e4m3fn).view(np.uint8)
    else:
        c = by_word.astype(ml_dtypes.float4_e2m1fn).view(np.uint8) & 0xF
        words = c[..., 0::2] | (c[..., 1::2] << 4)
    return np.ascontiguousarray(words), np.ascontiguousarray(byte.astype(np.uint8).reshape(k // 512, 16, n))


def unpack_weight(words, scales, fmt):
    g, p, n, _ = words.shape
    if fmt == "e4m3":
        vals = np.ascontiguousarray(words).view(ml_dtypes.float8_e4m3fn).astype(np.float64)
    else:
        nib = np.empty((g, p, n, 4), np.uint8)
        nib[..., 0::2] = words & 0xF
        nib[..., 1::2] = words >> 4
        vals = E2M1[nib]
    vals = vals * np.repeat(np.exp2(scales.astype(np.float64) - 127.0), 8, axis=1)[..., None]
    return vals.transpose(0, 1, 3, 2).reshape(g * 512, n)
def pack4(w):
    words, scales = pack_weight(w, "e2m1")
    return words.reshape(words.shape[0], 128, -1), scales


def unpack4(words, scales):
    return unpack_weight(words.reshape(words.shape[0], 128, -1, 2), scales, "e2m1")


E4M3FN = np.array([(-1.0 if i & 128 else 1.0) * ((1.0 + (i & 7) / 8.0) * 2.0 ** (((i >> 3) & 15) - 7) if i & 120 else (i & 7) * 2.0 ** -9) for i in range(256)])


def e4m3fn_bytes(y):
    return np.clip(np.asarray(y, np.float64), -448.0, 448.0).astype(np.float32).astype(ml_dtypes.float8_e4m3fn).view(np.uint8)


def e4m3fn_values(b):
    return E4M3FN[b]


T, L, A, V, D, BLK = 2048, 512, 4, 2048, 1024, 32


def setup_inputs():
    s = mx_kscale(T)
    tok = np.random.randint(0, A, (T // BLK, BLK, L))
    tok[:, :A] = (tok[:, :1] + np.arange(A)[:, None]) % A
    hot = (tok.reshape(T, L, 1) == np.arange(A)).reshape(T, V).astype(np.float64)
    H_words, H_scales = pack4(hot * s[:, None])
    size = np.exp(0.5 * np.random.standard_normal((T, 1)))
    G = np.random.standard_normal((T, D)) * size * np.sqrt(A / T) / s[:, None]
    G_scale = (np.abs(G).max(axis=1, keepdims=True) / 448.0).astype(np.float32)
    return {"H_words": H_words, "H_scales": H_scales,
            "G_bytes": e4m3fn_bytes(G / G_scale.astype(np.float64)),
            "G_scale": G_scale,
            "gamma": bf(1 + 0.1 * np.random.standard_normal(D)),
            "E": bf(np.random.standard_normal((V, D))),
            "lam": bf(np.random.uniform(0.2, 0.5, V))}


def reference(H_words, H_scales, G_bytes, G_scale, gamma, E, lam):
    H = unpack4(H_words, H_scales)
    G = e4m3fn_values(G_bytes) * np.repeat(f64(G_scale), D, axis=1)
    acc = H.T @ mxq(G, 0, "e4m3")
    return acc * f64(gamma) + f64(lam)[:, None] * f64(E)

@@ -1,0 +1,328 @@
+from contextlib import ExitStack
+
+import concourse.mybir as mybir
+from concourse.masks import make_identity
+
+T, V, D = 2048, 2048, 1024
+FLOPS = 2 * T * V * D
+
+F32 = mybir.dt.float32
+BF16 = mybir.dt.bfloat16
+I32 = mybir.dt.int32
+U32 = mybir.dt.uint32
+U8 = mybir.dt.uint8
+FP8 = mybir.dt.float8_e4m3fn
+E4M3X4 = mybir.dt.float8_e4m3fn_x4
+E2M1X4 = mybir.dt.float4_e2m1fn_x4
+MULT = mybir.AluOpType.mult
+ADD = mybir.AluOpType.add
+COPY = mybir.ActivationFunctionType.Copy
+
+P = 128
+PACK = 4
+GROUPS = T // (P * PACK)
+VT = V // P
+DB = D // P
+W = 512
+COLS = {"A": (0, 256), "C": (256, 256), "B": (512, 512)}
+WIDEN_V = {"A": (4,4,4,4), "B": (4,0,4,0), "C": (0,0,0,0)}
+EVAC_V = ((1, 0), (1, 0), (1, 0), (1, 0))
+MIX_V = {"A": (256,256,256,256), "B": (512,512,512,512), "C": (0,0,0,0)}
+
+
+def tile_onehot_embedding_table_gradient_d6_kernel(tc, H_words, H_scales, G_bytes, G_scale, gamma, E, lam, out):
+    nc = tc.nc
+    with ExitStack() as ctx:
+        keep = ctx.enter_context(tc.tile_pool(name="keep", bufs=1))
+        stage = ctx.enter_context(tc.tile_pool(name="stage", bufs=4))
+        psum = ctx.enter_context(tc.psum_pool(name="psum", bufs=8))
+        ctx.enter_context(tc.manual_schedule())
+
+        gs = keep.tile([P, GROUPS, PACK], F32, name="gs")
+        rows = keep.tile([P, P], BF16, name="rows")
+        ident = keep.tile([P, P], BF16, name="ident")
+        identf = keep.tile([P, P], F32, name="identf")
+        cols = keep.tile([P, VT + DB], F32, name="cols")
+        colsb = keep.tile([P, VT + DB], BF16, name="colsb")
+        gam = keep.tile([P, W], BF16, name="gam")
+        hs = keep.tile([P, GROUPS, V], U8, name="hs", align_bytes=64)
+        graw = [[keep.tile([P, PACK, W], U8, name=f"graw{g}_{s}", align_bytes=64) for s in range(2)] for g in range(GROUPS)]
+        hw = [keep.tile([P, 2 * V], U8, name=f"hw{g}", align_bytes=64) for g in range(GROUPS)]
+        et = [keep.tile([P, D], BF16, name=f"et{i}") for i in range(VT)]
+        codes = {}
+        scales = {}
+        for r, (c0, width) in COLS.items():
+            for g in range(GROUPS):
+                codes[r, g] = keep.tile([P, width], U32, name=f"codes{r}{g}", align_bytes=64)
+                scales[r, g] = keep.tile([P, width], U8, name=f"scales{r}{g}", align_bytes=64)
+
+        nc.gpsimd.memset(rows[:], 0.0)
+        make_identity(nc, ident[:])
+        for g in range(GROUPS):
+            eng = nc.vector if g < 2 else nc.gpsimd
+            eng.memset(hs[:, g, :].bitcast(I32), 0)
+        nc.scalar.activation(out=identf[:], in_=ident[:], func=COPY)
+
+        sbytes = H_scales.bitcast(I32)
+        words = H_words.bitcast(I32)
+
+        def load_g(g, s):
+            nc.sync.dma_start(
+                out=graw[g][s][:],
+                in_=G_bytes[g * 512 : (g + 1) * 512, s * W : (s + 1) * W].rearrange("(p t) n -> p t n", t=PACK),
+            )
+
+        def load_h(g):
+            nc.sync.dma_start(out=hw[g][:].bitcast(I32), in_=words[g])
+
+        def load_e(i):
+            nc.sync.dma_start(out=et[i][:], in_=E[i * P : (i + 1) * P, :])
+
+        nc.sync.dma_start(out=gs[:], in_=G_scale.rearrange("(g p t) o -> p g (t o)", p=P, t=PACK))
+        load_g(0, 0)
+        nc.sync.dma_start(out=rows[0:VT, :], in_=lam.rearrange("(i p) -> i p", p=P))
+        nc.sync.dma_start(out=rows[VT : VT + DB, :], in_=gamma.rearrange("(i p) -> i p", p=P))
+        load_h(0)
+        load_g(1, 0)
+        for Q in range(4):
+            nc.sync.dma_start(
+                out=hs[32 * Q : 32 * Q + 4, :, :].bitcast(I32),
+                in_=sbytes[:, 4 * Q : 4 * Q + 4, :].rearrange("g q n -> q g n"),
+            )
+        load_h(1)
+        load_g(2, 0)
+        load_g(3, 0)
+        load_h(2)
+        load_h(3)
+        load_g(0, 1)
+        load_g(1, 1)
+        load_g(2, 1)
+        load_g(3, 1)
+        for i in range(VT):
+            load_e(i)
+
+        def turn_rows():
+            tr = psum.tile([P, P], BF16, name="tr", tag="acc")
+            nc.tensor.transpose(tr[:], rows[:], ident[:])
+            nc.vector.tensor_copy(out=cols[:], in_=tr[:, 0 : VT + DB])
+            nc.vector.tensor_copy(out=colsb[:], in_=tr[:, 0 : VT + DB])
+
+        def spread_gamma():
+            gb = psum.tile([P, W], BF16, name="gb", tag="acc")
+            for b in range(W // P):
+                c = VT + W // P + b
+                nc.tensor.matmul(gb[:, b * P : (b + 1) * P], lhsT=colsb[:, c : c + 1].to_broadcast([P, P]), rhs=ident[:], start=True, stop=True)
+            nc.scalar.copy(out=gam[:], in_=gb[:])
+
+        wide = {}
+        mixed = {}
+
+        def widen(r, g):
+            c0, width = COLS[r]
+            s, c = divmod(c0, W)
+            wide[r, g] = stage.tile([P, PACK, width], BF16, name=f"wide{r}", align_bytes=64)
+            mixed[r, g] = stage.tile([P, width, PACK], BF16, name=f"mixed{r}", align_bytes=64)
+            for t in range(PACK):
+                src = graw[g][s][:, t, c : c + width].bitcast(FP8)
+                if t < WIDEN_V[r][g]:
+                    nc.vector.tensor_scalar(out=wide[r, g][:, t, :], in0=src, scalar1=gs[:, g, t : t + 1], scalar2=None, op0=MULT)
+                else:
+                    nc.scalar.activation(out=wide[r, g][:, t, :], in_=src, func=COPY, scale=gs[:, g, t : t + 1])
+
+        def interleave(r, g, part=None):
+            width = COLS[r][1]
+            c = MIX_V[r][g]
+            if part is not None:
+                src = wide[r, g][:].rearrange("p t n -> p n t")
+                nc.vector.tensor_copy(out=mixed[r, g][:, part * c // 2 : (part + 1) * c // 2, :], in_=src[:, part * c // 2 : (part + 1) * c // 2, :])
+                return
+            src = wide[r, g][:].rearrange("p t n -> p n t")
+            if c > 0:
+                nc.vector.tensor_copy(out=mixed[r, g][:, 0:c, :], in_=src[:, 0:c, :])
+            if c < width:
+                nc.scalar.copy(out=mixed[r, g][:, c:width, :], in_=src[:, c:width, :])
+
+        def quantize(r, g):
+            nc.vector.quantize_mx(
+                out=codes[r, g][:].bitcast(E4M3X4),
+                scales=scales[r, g][:],
+                in_=mixed[r, g][:].rearrange("p n t -> p (n t)"),
+            )
+
+        acc = {}
+        tmp = {}
+        turned = {}
+
+        def product(i, g):
+            if g == 0:
+                acc[i] = psum.tile([P, W], F32, name="acc", tag="acc")
+            nc.tensor.matmul_mx(
+                out=acc[i][:],
+                lhsT=hw[g][:, 2 * i * P : 2 * (i + 1) * P].bitcast(E2M1X4),
+                lhsT_scale=hs[:, g, i * P : (i + 1) * P],
+                rhs=codes["B", g][:].bitcast(E4M3X4),
+                rhs_scale=scales["B", g][:],
+                start=(g == 0),
+                stop=(g == GROUPS - 1),
+            )
+
+        def gain(i):
+            tmp[i] = stage.tile([P, W], F32, name="tmp")
+            nc.vector.tensor_tensor(out=tmp[i][:], in0=acc[i][:], in1=gam[:], op=MULT)
+
+        def decay(i):
+            res = stage.tile([P, W], F32, name="res", bufs=6)
+            nc.vector.scalar_tensor_tensor(out=res[:], in0=et[i][:, W:D], scalar=cols[:, i : i + 1], in1=tmp[i][:], op0=MULT, op1=ADD)
+            nc.sync.dma_start(out=out[i * P : (i + 1) * P, W:D], in_=res[:])
+
+        accT = {}
+        gained = {}
+
+        def productT(r, q, b, g):
+            if g == 0:
+                accT[r, q, b] = psum.tile([P, W], F32, name="accT", tag="acc")
+            nc.tensor.matmul_mx(
+                out=accT[r, q, b][:],
+                lhsT=codes[r, g][:, b * P : (b + 1) * P].bitcast(E4M3X4),
+                lhsT_scale=scales[r, g][:, b * P : (b + 1) * P],
+                rhs=hw[g][:, 2 * q * W : 2 * (q + 1) * W].bitcast(E2M1X4),
+                rhs_scale=hs[:, g, q * W : (q + 1) * W],
+                start=(g == 0),
+                stop=(g == GROUPS - 1),
+            )
+
+        def gainT(r, q, b, on_vector=False):
+            gained[r, q, b] = stage.tile([P, W], F32, name="gained", bufs=10)
+            c = VT + COLS[r][0] // P + b
+            if on_vector:
+                nc.vector.tensor_scalar(out=gained[r, q, b][:], in0=accT[r, q, b][:], scalar1=cols[:, c : c + 1], scalar2=None, op0=MULT)
+            else:
+                nc.scalar.activation(out=gained[r, q, b][:], in_=accT[r, q, b][:], func=COPY, scale=cols[:, c : c + 1])
+
+        def turn(r, i):
+            q, j = divmod(i, 4)
+            width = COLS[r][1]
+            turned[r, i] = psum.tile([P, W // width, width], F32, name="turned", tag="acc")
+            for k in range(W // width):
+                for b in range(width // P):
+                    nc.tensor.transpose(turned[r, i][:, k, b * P : (b + 1) * P], gained[r, q, b][:, (j + k) * P : (j + k + 1) * P], identf[:])
+
+        def decayT(r, i):
+            c0, width = COLS[r]
+            for k in range(W // width):
+                res = stage.tile([P, width], F32, name=f"res{r}", bufs=8)
+                nc.vector.scalar_tensor_tensor(
+                    out=res[:], in0=et[i + k][:, c0 : c0 + width], scalar=cols[:, i + k : i + k + 1], in1=turned[r, i][:, k, :], op0=MULT, op1=ADD
+                )
+                nc.sync.dma_start(out=out[(i + k) * P : (i + k + 1) * P, c0 : c0 + width], in_=res[:])
+
+        def pairs(q):
+            return range(4 * q, 4 * q + 4, 2)
+
+        def roundT(r, q):
+            for b in range(2):
+                for g in range(GROUPS):
+                    productT(r, q, b, g)
+
+        def turns(r, q):
+            for i in pairs(q):
+                turn(r, i)
+
+        def decays(r, q):
+            for i in pairs(q):
+                decayT(r, i)
+
+        def rows_of(i):
+            for g in range(GROUPS):
+                product(i, g)
+
+        def finish(i):
+            gain(i)
+            gain(i + 1)
+            decay(i)
+            decay(i + 1)
+
+        widen("A", 0)
+        turn_rows()
+        interleave("A", 0)
+        quantize("A", 0)
+        widen("C", 0)
+        widen("A", 1)
+        interleave("C", 0)
+        interleave("A", 1)
+        widen("C", 1)
+        widen("A", 2)
+        quantize("A", 1)
+        interleave("C", 1)
+        interleave("A", 2)
+        widen("C", 2)
+        widen("A", 3)
+        quantize("A", 2)
+        interleave("C", 2)
+        interleave("A", 3)
+        quantize("C", 0)
+        quantize("A", 3)
+        quantize("C", 1)
+        widen("C", 3)
+        interleave("C", 3)
+        for g in range(GROUPS):
+            for q in range(4):
+                for b in range(2):
+                    productT("A", q, b, g)
+        widen("B", 0)
+        for q in range(4):
+            for b in range(2):
+                gainT("A", q, b, EVAC_V[q][b])
+            if q == 0:
+                quantize("C", 2)
+            if q == 1:
+                quantize("C", 3)
+        turns("A", 0)
+        roundT("C", 0)
+        turns("A", 1)
+        interleave("B", 0)
+        decays("A", 0)
+        quantize("B", 0)
+        roundT("C", 1)
+        for b in range(2):
+            gainT("C", 0, b)
+        widen("B", 1)
+        turns("A", 2)
+        decays("A", 1)
+        roundT("C", 2)
+        interleave("B", 1)
+        decays("A", 2)
+        quantize("B", 1)
+        for b in range(2):
+            gainT("C", 1, b)
+        widen("B", 2)
+        turns("A", 3)
+        decays("A", 3)
+        interleave("B", 2)
+        for b in range(2):
+            gainT("C", 2, b)
+        turns("C", 0)
+        decays("C", 0)
+        quantize("B", 2)
+        widen("B", 3)
+        roundT("C", 3)
+        turns("C", 1)
+        decays("C", 1)
+        interleave("B", 3)
+        spread_gamma()
+        for b in range(2):
+            gainT("C", 3, b)
+        turns("C", 2)
+        decays("C", 2)
+        quantize("B", 3)
+        for g in range(GROUPS):
+            for i in range(4):
+                product(i, g)
+        finish(0)
+        finish(2)
+        for i in range(4, 16):
+            rows_of(i)
+        for i in range(4, 16, 2):
+            finish(i)
+        turns("C", 3)
+        decays("C", 3)

@@ -24,10 +24,10 @@ GROUPS = T // (P * PACK)
 VT = V // P
 DB = D // P
 W = 512
-COLS = {"A": (0, 256), "C": (256, 256), "B": (512, 512)}
-WIDEN_V = {"A": (4,4,4,4), "B": (4,0,4,0), "C": (0,0,0,0)}
-EVAC_V = ((1, 0), (1, 0), (1, 0), (1, 0))
-MIX_V = {"A": (256,256,256,256), "B": (512,512,512,512), "C": (0,0,0,0)}
+COLS = {"A": (0, 512), "B": (512, 512)}
+WIDEN_V = {"A":[4,0,4,2],"B":[2,2,1,4]}
+MIX_V = {"A":[512,128,512,0],"B":[384,448,0,512]}
+EVAC_V = {"A00":0,"A01":0,"A02":1,"A03":0,"A10":1,"A11":0,"A12":0,"A13":0,"A20":1,"A21":1,"A22":0,"A23":1,"A30":1,"A31":0,"A32":0,"A33":0,"B00":0,"B01":0,"B02":0,"B03":1,"B10":1,"B11":1,"B12":1,"B13":0,"B20":0,"B21":1,"B22":0,"B23":1,"B30":0,"B31":0,"B32":0,"B33":0}
 
 
 def tile_onehot_embedding_table_gradient_d6_kernel(tc, H_words, H_scales, G_bytes, G_scale, gamma, E, lam, out):
@@ -38,17 +38,17 @@ def tile_onehot_embedding_table_gradient_d6_kernel(tc, H_words, H_scales, G_byte
         psum = ctx.enter_context(tc.psum_pool(name="psum", bufs=8))
         ctx.enter_context(tc.manual_schedule())
 
-        gs = keep.tile([P, GROUPS, PACK], F32, name="gs")
+        gs = keep.tile([P, GROUPS, 2 * PACK], F32, name="gs")
         rows = keep.tile([P, P], BF16, name="rows")
         ident = keep.tile([P, P], BF16, name="ident")
         identf = keep.tile([P, P], F32, name="identf")
         cols = keep.tile([P, VT + DB], F32, name="cols")
         colsb = keep.tile([P, VT + DB], BF16, name="colsb")
         gam = keep.tile([P, W], BF16, name="gam")
-        hs = keep.tile([P, GROUPS, V], U8, name="hs", align_bytes=64)
-        graw = [[keep.tile([P, PACK, W], U8, name=f"graw{g}_{s}", align_bytes=64) for s in range(2)] for g in range(GROUPS)]
-        hw = [keep.tile([P, 2 * V], U8, name=f"hw{g}", align_bytes=64) for g in range(GROUPS)]
-        et = [keep.tile([P, D], BF16, name=f"et{i}") for i in range(VT)]
+        hs = [keep.tile([P, V], U8, name=f"hs{g}", align_bytes=64) for g in range(GROUPS)]
+        graw = [keep.tile([P, PACK, D], U8, name=f"graw{g}", align_bytes=64) for g in range(GROUPS)]
+        hw = [[keep.tile([P, V], U8, name=f"hw{g}_{s}", align_bytes=64) for s in range(2)] for g in range(GROUPS)]
+        et = [keep.tile([P, 2, D], BF16, name=f"et{i}") for i in range(VT // 2)]
         codes = {}
         scales = {}
         for r, (c0, width) in COLS.items():
@@ -56,50 +56,37 @@ def tile_onehot_embedding_table_gradient_d6_kernel(tc, H_words, H_scales, G_byte
                 codes[r, g] = keep.tile([P, width], U32, name=f"codes{r}{g}", align_bytes=64)
                 scales[r, g] = keep.tile([P, width], U8, name=f"scales{r}{g}", align_bytes=64)
 
-        nc.gpsimd.memset(rows[:], 0.0)
-        make_identity(nc, ident[:])
         for g in range(GROUPS):
             eng = nc.vector if g < 2 else nc.gpsimd
-            eng.memset(hs[:, g, :].bitcast(I32), 0)
+            eng.memset(hs[g][:].bitcast(I32), 0)
+        nc.gpsimd.memset(rows[:], 0.0)
+        make_identity(nc, ident[:])
         nc.scalar.activation(out=identf[:], in_=ident[:], func=COPY)
 
         sbytes = H_scales.bitcast(I32)
         words = H_words.bitcast(I32)
 
-        def load_g(g, s):
-            nc.sync.dma_start(
-                out=graw[g][s][:],
-                in_=G_bytes[g * 512 : (g + 1) * 512, s * W : (s + 1) * W].rearrange("(p t) n -> p t n", t=PACK),
-            )
-
-        def load_h(g):
-            nc.sync.dma_start(out=hw[g][:].bitcast(I32), in_=words[g])
-
-        def load_e(i):
-            nc.sync.dma_start(out=et[i][:], in_=E[i * P : (i + 1) * P, :])
-
-        nc.sync.dma_start(out=gs[:], in_=G_scale.rearrange("(g p t) o -> p g (t o)", p=P, t=PACK))
-        load_g(0, 0)
-        nc.sync.dma_start(out=rows[0:VT, :], in_=lam.rearrange("(i p) -> i p", p=P))
-        nc.sync.dma_start(out=rows[VT : VT + DB, :], in_=gamma.rearrange("(i p) -> i p", p=P))
-        load_h(0)
-        load_g(1, 0)
-        for Q in range(4):
-            nc.sync.dma_start(
-                out=hs[32 * Q : 32 * Q + 4, :, :].bitcast(I32),
-                in_=sbytes[:, 4 * Q : 4 * Q + 4, :].rearrange("g q n -> q g n"),
-            )
-        load_h(1)
-        load_g(2, 0)
-        load_g(3, 0)
-        load_h(2)
-        load_h(3)
-        load_g(0, 1)
-        load_g(1, 1)
-        load_g(2, 1)
-        load_g(3, 1)
-        for i in range(VT):
-            load_e(i)
+        def load(x):
+            k = x[0]
+            n = int(x[1:])
+            if k == "S":
+                nc.sync.dma_start(out=gs[:, n, 0:PACK], in_=G_scale[n * 512 : (n + 1) * 512, :].rearrange("(p t) o -> p (t o)", t=PACK))
+            elif k == "G":
+                nc.sync.dma_start(out=graw[n][:].rearrange("p t n -> p (t n)"), in_=G_bytes[n * 512 : (n + 1) * 512, :].rearrange("(p t) n -> p (t n)", t=PACK))
+            elif k in "HJ":
+                s = 0 if k == "H" else 1
+                nc.sync.dma_start(out=hw[n][s][:].bitcast(I32), in_=words[n, :, s * V // 4 : (s + 1) * V // 4])
+            elif k == "R":
+                nc.sync.dma_start(out=rows[0:VT, :], in_=lam.rearrange("(i p) -> i p", p=P))
+                nc.sync.dma_start(out=rows[VT : VT + DB, :], in_=gamma.rearrange("(i p) -> i p", p=P))
+            elif k == "Q":
+                for Q in range(4):
+                    nc.sync.dma_start(
+                        out=hs[n][32 * Q : 32 * Q + 4, :].bitcast(I32),
+                        in_=sbytes[n, 4 * Q : 4 * Q + 4, :],
+                    )
+            else:
+                nc.sync.dma_start(out=et[n][:], in_=E[2 * n * P : 2 * (n + 1) * P, :].rearrange("(k p) d -> p k d", p=P))
 
         def turn_rows():
             tr = psum.tile([P, P], BF16, name="tr", tag="acc")
@@ -119,28 +106,24 @@ def tile_onehot_embedding_table_gradient_d6_kernel(tc, H_words, H_scales, G_byte
 
         def widen(r, g):
             c0, width = COLS[r]
-            s, c = divmod(c0, W)
             wide[r, g] = stage.tile([P, PACK, width], BF16, name=f"wide{r}", align_bytes=64)
-            mixed[r, g] = stage.tile([P, width, PACK], BF16, name=f"mixed{r}", align_bytes=64)
             for t in range(PACK):
-                src = graw[g][s][:, t, c : c + width].bitcast(FP8)
+                src = graw[g][:, t, c0 : c0 + width].bitcast(FP8)
                 if t < WIDEN_V[r][g]:
                     nc.vector.tensor_scalar(out=wide[r, g][:, t, :], in0=src, scalar1=gs[:, g, t : t + 1], scalar2=None, op0=MULT)
                 else:
                     nc.scalar.activation(out=wide[r, g][:, t, :], in_=src, func=COPY, scale=gs[:, g, t : t + 1])
 
-        def interleave(r, g, part=None):
+        def interleave(r, g):
             width = COLS[r][1]
             c = MIX_V[r][g]
-            if part is not None:
-                src = wide[r, g][:].rearrange("p t n -> p n t")
-                nc.vector.tensor_copy(out=mixed[r, g][:, part * c // 2 : (part + 1) * c // 2, :], in_=src[:, part * c // 2 : (part + 1) * c // 2, :])
-                return
-            src = wide[r, g][:].rearrange("p t n -> p n t")
+            mixed[r, g] = stage.tile([P, width, PACK], BF16, name=f"mixed{r}", align_bytes=64)
+            dst = mixed[r, g][:].rearrange("p (c i) t -> p c t i", i=4)
+            src = wide[r, g][:].rearrange("p t (c i) -> p c t i", i=4)
             if c > 0:
-                nc.vector.tensor_copy(out=mixed[r, g][:, 0:c, :], in_=src[:, 0:c, :])
+                nc.vector.tensor_copy(out=dst[:, 0 : c // 4], in_=src[:, 0 : c // 4])
             if c < width:
-                nc.scalar.copy(out=mixed[r, g][:, c:width, :], in_=src[:, c:width, :])
+                nc.scalar.copy(out=dst[:, c // 4 : width // 4], in_=src[:, c // 4 : width // 4])
 
         def quantize(r, g):
             nc.vector.quantize_mx(
@@ -158,22 +141,26 @@ def tile_onehot_embedding_table_gradient_d6_kernel(tc, H_words, H_scales, G_byte
                 acc[i] = psum.tile([P, W], F32, name="acc", tag="acc")
             nc.tensor.matmul_mx(
                 out=acc[i][:],
-                lhsT=hw[g][:, 2 * i * P : 2 * (i + 1) * P].bitcast(E2M1X4),
-                lhsT_scale=hs[:, g, i * P : (i + 1) * P],
+                lhsT=hw[g][i // 8][:, 2 * (i % 8) * P : 2 * (i % 8 + 1) * P].bitcast(E2M1X4),
+                lhsT_scale=hs[g][:, i * P : (i + 1) * P],
                 rhs=codes["B", g][:].bitcast(E4M3X4),
                 rhs_scale=scales["B", g][:],
                 start=(g == 0),
                 stop=(g == GROUPS - 1),
             )
 
+        def rows_of(i):
+            for g in range(GROUPS):
+                product(i, g)
+
         def gain(i):
             tmp[i] = stage.tile([P, W], F32, name="tmp")
             nc.vector.tensor_tensor(out=tmp[i][:], in0=acc[i][:], in1=gam[:], op=MULT)
 
         def decay(i):
-            res = stage.tile([P, W], F32, name="res", bufs=6)
-            nc.vector.scalar_tensor_tensor(out=res[:], in0=et[i][:, W:D], scalar=cols[:, i : i + 1], in1=tmp[i][:], op0=MULT, op1=ADD)
-            nc.sync.dma_start(out=out[i * P : (i + 1) * P, W:D], in_=res[:])
+            o = stage.tile([P, W], F32, name="resB", bufs=6)
+            nc.vector.scalar_tensor_tensor(out=o[:], in0=et[i // 2][:, i % 2, W:D], scalar=cols[:, i : i + 1], in1=tmp[i][:], op0=MULT, op1=ADD)
+            nc.sync.dma_start(out=out[i * P : (i + 1) * P, W:D], in_=o[:])
 
         accT = {}
         gained = {}
@@ -185,144 +172,219 @@ def tile_onehot_embedding_table_gradient_d6_kernel(tc, H_words, H_scales, G_byte
                 out=accT[r, q, b][:],
                 lhsT=codes[r, g][:, b * P : (b + 1) * P].bitcast(E4M3X4),
                 lhsT_scale=scales[r, g][:, b * P : (b + 1) * P],
-                rhs=hw[g][:, 2 * q * W : 2 * (q + 1) * W].bitcast(E2M1X4),
-                rhs_scale=hs[:, g, q * W : (q + 1) * W],
+                rhs=hw[g][q // 2][:, 2 * (q % 2) * W : 2 * (q % 2 + 1) * W].bitcast(E2M1X4),
+                rhs_scale=hs[g][:, q * W : (q + 1) * W],
                 start=(g == 0),
                 stop=(g == GROUPS - 1),
             )
 
-        def gainT(r, q, b, on_vector=False):
-            gained[r, q, b] = stage.tile([P, W], F32, name="gained", bufs=10)
+        def roundA(g):
+            for q in range(2):
+                for b in range(4):
+                    productT("A", q, b, g)
+
+        def roundT(r, q, b):
+            for g in range(GROUPS):
+                productT(r, q, b, g)
+
+        def gainT(r, q, b):
+            gained[r, q, b] = stage.tile([P, W], F32, name="gained", bufs=12)
             c = VT + COLS[r][0] // P + b
-            if on_vector:
+            if EVAC_V[f"{r}{q}{b}"]:
                 nc.vector.tensor_scalar(out=gained[r, q, b][:], in0=accT[r, q, b][:], scalar1=cols[:, c : c + 1], scalar2=None, op0=MULT)
             else:
                 nc.scalar.activation(out=gained[r, q, b][:], in_=accT[r, q, b][:], func=COPY, scale=cols[:, c : c + 1])
 
         def turn(r, i):
             q, j = divmod(i, 4)
-            width = COLS[r][1]
-            turned[r, i] = psum.tile([P, W // width, width], F32, name="turned", tag="acc")
-            for k in range(W // width):
-                for b in range(width // P):
-                    nc.tensor.transpose(turned[r, i][:, k, b * P : (b + 1) * P], gained[r, q, b][:, (j + k) * P : (j + k + 1) * P], identf[:])
+            turned[r, i] = psum.tile([P, W], F32, name="turned", tag="acc")
+            for b in range(W // P):
+                nc.tensor.transpose(turned[r, i][:, b * P : (b + 1) * P], gained[r, q, b][:, j * P : (j + 1) * P], identf[:])
 
         def decayT(r, i):
             c0, width = COLS[r]
-            for k in range(W // width):
-                res = stage.tile([P, width], F32, name=f"res{r}", bufs=8)
-                nc.vector.scalar_tensor_tensor(
-                    out=res[:], in0=et[i + k][:, c0 : c0 + width], scalar=cols[:, i + k : i + k + 1], in1=turned[r, i][:, k, :], op0=MULT, op1=ADD
-                )
-                nc.sync.dma_start(out=out[(i + k) * P : (i + k + 1) * P, c0 : c0 + width], in_=res[:])
+            o = stage.tile([P, W], F32, name="resB", bufs=6)
+            nc.vector.scalar_tensor_tensor(
+                out=o[:], in0=et[i // 2][:, i % 2, c0 : c0 + W], scalar=cols[:, i : i + 1], in1=turned[r, i][:], op0=MULT, op1=ADD
+            )
+            nc.sync.dma_start(out=out[i * P : (i + 1) * P, c0 : c0 + W], in_=o[:])
 
-        def pairs(q):
-            return range(4 * q, 4 * q + 4, 2)
-
-        def roundT(r, q):
-            for b in range(2):
-                for g in range(GROUPS):
-                    productT(r, q, b, g)
-
-        def turns(r, q):
-            for i in pairs(q):
-                turn(r, i)
-
-        def decays(r, q):
-            for i in pairs(q):
-                decayT(r, i)
-
-        def rows_of(i):
-            for g in range(GROUPS):
-                product(i, g)
-
-        def finish(i):
-            gain(i)
-            gain(i + 1)
-            decay(i)
-            decay(i + 1)
-
-        widen("A", 0)
-        turn_rows()
-        interleave("A", 0)
-        quantize("A", 0)
-        widen("C", 0)
+        load("G0")
+        load("S0")
+        load("G1")
+        load("S1")
+        load("Q0")
+        load("R0")
+        load("G3")
+        load("S2")
+        load("H0")
+        load("S3")
+        load("G2")
+        load("H1")
+        load("Q1")
+        load("J2")
+        load("H2")
+        load("Q2")
+        load("J0")
+        load("H3")
+        load("Q3")
+        load("J3")
+        load("J1")
+        load("E2")
+        load("E1")
+        load("E5")
+        load("E0")
+        load("E3")
+        load("E7")
+        load("E6")
+        load("E4")
         widen("A", 1)
-        interleave("C", 0)
+        widen("A", 0)
+        interleave("A", 0)
+        turn_rows()
+        quantize("A", 0)
         interleave("A", 1)
-        widen("C", 1)
+        widen("A", 3)
+        roundA(0)
         widen("A", 2)
         quantize("A", 1)
-        interleave("C", 1)
+        roundA(1)
         interleave("A", 2)
-        widen("C", 2)
-        widen("A", 3)
         quantize("A", 2)
-        interleave("C", 2)
+        roundA(2)
         interleave("A", 3)
-        quantize("C", 0)
         quantize("A", 3)
-        quantize("C", 1)
-        widen("C", 3)
-        interleave("C", 3)
-        for g in range(GROUPS):
-            for q in range(4):
-                for b in range(2):
-                    productT("A", q, b, g)
+        roundA(3)
+        roundT("A", 2, 1)
         widen("B", 0)
-        for q in range(4):
-            for b in range(2):
-                gainT("A", q, b, EVAC_V[q][b])
-            if q == 0:
-                quantize("C", 2)
-            if q == 1:
-                quantize("C", 3)
-        turns("A", 0)
-        roundT("C", 0)
-        turns("A", 1)
-        interleave("B", 0)
-        decays("A", 0)
-        quantize("B", 0)
-        roundT("C", 1)
-        for b in range(2):
-            gainT("C", 0, b)
         widen("B", 1)
-        turns("A", 2)
-        decays("A", 1)
-        roundT("C", 2)
-        interleave("B", 1)
-        decays("A", 2)
-        quantize("B", 1)
-        for b in range(2):
-            gainT("C", 1, b)
-        widen("B", 2)
-        turns("A", 3)
-        decays("A", 3)
-        interleave("B", 2)
-        for b in range(2):
-            gainT("C", 2, b)
-        turns("C", 0)
-        decays("C", 0)
-        quantize("B", 2)
+        gainT("A", 1, 0)
+        gainT("A", 0, 3)
+        roundT("A", 2, 2)
+        roundT("A", 2, 0)
+        gainT("A", 1, 3)
+        interleave("B", 0)
+        roundT("A", 3, 0)
         widen("B", 3)
-        roundT("C", 3)
-        turns("C", 1)
-        decays("C", 1)
-        interleave("B", 3)
+        gainT("A", 0, 0)
+        gainT("A", 0, 2)
+        gainT("A", 1, 2)
+        widen("B", 2)
+        roundT("A", 3, 2)
+        gainT("A", 2, 1)
+        quantize("B", 0)
+        interleave("B", 1)
+        gainT("A", 0, 1)
+        turn("A", 0)
+        gainT("A", 2, 2)
+        gainT("A", 1, 1)
+        roundT("A", 2, 3)
+        turn("A", 2)
+        gainT("A", 3, 2)
+        decayT("A", 0)
         spread_gamma()
-        for b in range(2):
-            gainT("C", 3, b)
-        turns("C", 2)
-        decays("C", 2)
+        quantize("B", 1)
+        turn("A", 1)
+        turn("A", 3)
+        turn("A", 6)
+        gainT("A", 2, 0)
+        decayT("A", 2)
+        turn("A", 5)
+        roundT("A", 3, 3)
+        decayT("A", 3)
+        product(3, 0)
+        product(0, 0)
+        interleave("B", 2)
+        roundT("A", 3, 1)
+        product(2, 0)
+        gainT("A", 3, 0)
+        product(1, 0)
+        gainT("A", 2, 3)
+        gainT("A", 3, 3)
+        product(1, 1)
+        turn("A", 4)
+        turn("A", 7)
+        turn("A", 9)
+        decayT("A", 5)
+        turn("A", 11)
+        decayT("A", 6)
+        product(3, 1)
+        quantize("B", 2)
+        product(1, 2)
+        decayT("A", 1)
+        product(0, 1)
+        product(3, 2)
+        product(0, 2)
+        product(2, 1)
+        gainT("A", 3, 1)
+        interleave("B", 3)
+        product(2, 2)
+        turn("A", 8)
+        decayT("A", 4)
+        decayT("A", 9)
+        decayT("A", 7)
+        turn("A", 10)
+        turn("A", 12)
         quantize("B", 3)
-        for g in range(GROUPS):
-            for i in range(4):
-                product(i, g)
-        finish(0)
-        finish(2)
-        for i in range(4, 16):
-            rows_of(i)
-        for i in range(4, 16, 2):
-            finish(i)
-        turns("C", 3)
-        decays("C", 3)
+        turn("A", 15)
+        product(1, 3)
+        decayT("A", 11)
+        decayT("A", 8)
+        product(3, 3)
+        product(0, 3)
+        product(2, 3)
+        rows_of(6)
+        turn("A", 14)
+        turn("A", 13)
+        rows_of(5)
+        decayT("A", 10)
+        roundT("B", 3, 1)
+        decayT("A", 12)
+        rows_of(9)
+        gain(3)
+        gainT("B", 3, 1)
+        gain(2)
+        rows_of(4)
+        decayT("A", 15)
+        roundT("B", 3, 2)
+        gain(0)
+        decay(2)
+        gain(1)
+        decay(0)
+        decay(1)
+        rows_of(7)
+        gain(5)
+        gainT("B", 3, 2)
+        roundT("B", 3, 0)
+        decayT("A", 13)
+        decayT("A", 14)
+        decay(5)
+        gainT("B", 3, 0)
+        roundT("B", 3, 3)
+        gain(9)
+        gain(6)
+        rows_of(10)
+        gainT("B", 3, 3)
+        decay(3)
+        decay(6)
+        decay(9)
+        turn("B", 13)
+        turn("B", 12)
+        gain(7)
+        rows_of(11)
+        gain(4)
+        decay(7)
+        turn("B", 15)
+        decay(4)
+        gain(10)
+        decayT("B", 13)
+        rows_of(8)
+        decayT("B", 12)
+        decay(10)
+        gain(11)
+        decayT("B", 15)
+        decay(11)
+        turn("B", 14)
+        gain(8)
+        decayT("B", 14)
+        decay(8)

from contextlib import ExitStack

import concourse.mybir as mybir
from concourse.masks import make_identity

T, V, D = 2048, 2048, 1024
FLOPS = 2 * T * V * D

F32 = mybir.dt.float32
BF16 = mybir.dt.bfloat16
I32 = mybir.dt.int32
U32 = mybir.dt.uint32
U8 = mybir.dt.uint8
FP8 = mybir.dt.float8_e4m3fn
E4M3X4 = mybir.dt.float8_e4m3fn_x4
E2M1X4 = mybir.dt.float4_e2m1fn_x4
MULT = mybir.AluOpType.mult
ADD = mybir.AluOpType.add
COPY = mybir.ActivationFunctionType.Copy

P = 128
PACK = 4
GROUPS = T // (P * PACK)
VT = V // P
DB = D // P
W = 512
COLS = {"A": (0, 512), "B": (512, 512)}
WIDEN_V = {"A":[4,0,4,2],"B":[2,2,1,4]}
MIX_V = {"A":[512,128,512,0],"B":[384,448,0,512]}
EVAC_V = {"A00":0,"A01":0,"A02":1,"A03":0,"A10":1,"A11":0,"A12":0,"A13":0,"A20":1,"A21":1,"A22":0,"A23":1,"A30":1,"A31":0,"A32":0,"A33":0,"B00":0,"B01":0,"B02":0,"B03":1,"B10":1,"B11":1,"B12":1,"B13":0,"B20":0,"B21":1,"B22":0,"B23":1,"B30":0,"B31":0,"B32":0,"B33":0}


def tile_onehot_embedding_table_gradient_d6_kernel(tc, H_words, H_scales, G_bytes, G_scale, gamma, E, lam, out):
    nc = tc.nc
    with ExitStack() as ctx:
        keep = ctx.enter_context(tc.tile_pool(name="keep", bufs=1))
        stage = ctx.enter_context(tc.tile_pool(name="stage", bufs=4))
        psum = ctx.enter_context(tc.psum_pool(name="psum", bufs=8))
        ctx.enter_context(tc.manual_schedule())

        gs = keep.tile([P, GROUPS, 2 * PACK], F32, name="gs")
        rows = keep.tile([P, P], BF16, name="rows")
        ident = keep.tile([P, P], BF16, name="ident")
        identf = keep.tile([P, P], F32, name="identf")
        cols = keep.tile([P, VT + DB], F32, name="cols")
        colsb = keep.tile([P, VT + DB], BF16, name="colsb")
        gam = keep.tile([P, W], BF16, name="gam")
        hs = [keep.tile([P, V], U8, name=f"hs{g}", align_bytes=64) for g in range(GROUPS)]
        graw = [keep.tile([P, PACK, D], U8, name=f"graw{g}", align_bytes=64) for g in range(GROUPS)]
        hw = [[keep.tile([P, V], U8, name=f"hw{g}_{s}", align_bytes=64) for s in range(2)] for g in range(GROUPS)]
        et = [keep.tile([P, 2, D], BF16, name=f"et{i}") for i in range(VT // 2)]
        codes = {}
        scales = {}
        for r, (c0, width) in COLS.items():
            for g in range(GROUPS):
                codes[r, g] = keep.tile([P, width], U32, name=f"codes{r}{g}", align_bytes=64)
                scales[r, g] = keep.tile([P, width], U8, name=f"scales{r}{g}", align_bytes=64)

        for g in range(GROUPS):
            eng = nc.vector if g < 2 else nc.gpsimd
            eng.memset(hs[g][:].bitcast(I32), 0)
        nc.gpsimd.memset(rows[:], 0.0)
        make_identity(nc, ident[:])
        nc.scalar.activation(out=identf[:], in_=ident[:], func=COPY)

        sbytes = H_scales.bitcast(I32)
        words = H_words.bitcast(I32)

        def load(x):
            k = x[0]
            n = int(x[1:])
            if k == "S":
                nc.sync.dma_start(out=gs[:, n, 0:PACK], in_=G_scale[n * 512 : (n + 1) * 512, :].rearrange("(p t) o -> p (t o)", t=PACK))
            elif k == "G":
                nc.sync.dma_start(out=graw[n][:].rearrange("p t n -> p (t n)"), in_=G_bytes[n * 512 : (n + 1) * 512, :].rearrange("(p t) n -> p (t n)", t=PACK))
            elif k in "HJ":
                s = 0 if k == "H" else 1
                nc.sync.dma_start(out=hw[n][s][:].bitcast(I32), in_=words[n, :, s * V // 4 : (s + 1) * V // 4])
            elif k == "R":
                nc.sync.dma_start(out=rows[0:VT, :], in_=lam.rearrange("(i p) -> i p", p=P))
                nc.sync.dma_start(out=rows[VT : VT + DB, :], in_=gamma.rearrange("(i p) -> i p", p=P))
            elif k == "Q":
                for Q in range(4):
                    nc.sync.dma_start(
                        out=hs[n][32 * Q : 32 * Q + 4, :].bitcast(I32),
                        in_=sbytes[n, 4 * Q : 4 * Q + 4, :],
                    )
            else:
                nc.sync.dma_start(out=et[n][:], in_=E[2 * n * P : 2 * (n + 1) * P, :].rearrange("(k p) d -> p k d", p=P))

        def turn_rows():
            tr = psum.tile([P, P], BF16, name="tr", tag="acc")
            nc.tensor.transpose(tr[:], rows[:], ident[:])
            nc.vector.tensor_copy(out=cols[:], in_=tr[:, 0 : VT + DB])
            nc.vector.tensor_copy(out=colsb[:], in_=tr[:, 0 : VT + DB])

        def spread_gamma():
            gb = psum.tile([P, W], BF16, name="gb", tag="acc")
            for b in range(W // P):
                c = VT + W // P + b
                nc.tensor.matmul(gb[:, b * P : (b + 1) * P], lhsT=colsb[:, c : c + 1].to_broadcast([P, P]), rhs=ident[:], start=True, stop=True)
            nc.scalar.copy(out=gam[:], in_=gb[:])

        wide = {}
        mixed = {}

        def widen(r, g):
            c0, width = COLS[r]
            wide[r, g] = stage.tile([P, PACK, width], BF16, name=f"wide{r}", align_bytes=64)
            for t in range(PACK):
                src = graw[g][:, t, c0 : c0 + width].bitcast(FP8)
                if t < WIDEN_V[r][g]:
                    nc.vector.tensor_scalar(out=wide[r, g][:, t, :], in0=src, scalar1=gs[:, g, t : t + 1], scalar2=None, op0=MULT)
                else:
                    nc.scalar.activation(out=wide[r, g][:, t, :], in_=src, func=COPY, scale=gs[:, g, t : t + 1])

        def interleave(r, g):
            width = COLS[r][1]
            c = MIX_V[r][g]
            mixed[r, g] = stage.tile([P, width, PACK], BF16, name=f"mixed{r}", align_bytes=64)
            dst = mixed[r, g][:].rearrange("p (c i) t -> p c t i", i=4)
            src = wide[r, g][:].rearrange("p t (c i) -> p c t i", i=4)
            if c > 0:
                nc.vector.tensor_copy(out=dst[:, 0 : c // 4], in_=src[:, 0 : c // 4])
            if c < width:
                nc.scalar.copy(out=dst[:, c // 4 : width // 4], in_=src[:, c // 4 : width // 4])

        def quantize(r, g):
            nc.vector.quantize_mx(
                out=codes[r, g][:].bitcast(E4M3X4),
                scales=scales[r, g][:],
                in_=mixed[r, g][:].rearrange("p n t -> p (n t)"),
            )

        acc = {}
        tmp = {}
        turned = {}

        def product(i, g):
            if g == 0:
                acc[i] = psum.tile([P, W], F32, name="acc", tag="acc")
            nc.tensor.matmul_mx(
                out=acc[i][:],
                lhsT=hw[g][i // 8][:, 2 * (i % 8) * P : 2 * (i % 8 + 1) * P].bitcast(E2M1X4),
                lhsT_scale=hs[g][:, i * P : (i + 1) * P],
                rhs=codes["B", g][:].bitcast(E4M3X4),
                rhs_scale=scales["B", g][:],
                start=(g == 0),
                stop=(g == GROUPS - 1),
            )

        def rows_of(i):
            for g in range(GROUPS):
                product(i, g)

        def gain(i):
            tmp[i] = stage.tile([P, W], F32, name="tmp")
            nc.vector.tensor_tensor(out=tmp[i][:], in0=acc[i][:], in1=gam[:], op=MULT)

        def decay(i):
            o = stage.tile([P, W], F32, name="resB", bufs=6)
            nc.vector.scalar_tensor_tensor(out=o[:], in0=et[i // 2][:, i % 2, W:D], scalar=cols[:, i : i + 1], in1=tmp[i][:], op0=MULT, op1=ADD)
            nc.sync.dma_start(out=out[i * P : (i + 1) * P, W:D], in_=o[:])

        accT = {}
        gained = {}

        def productT(r, q, b, g):
            if g == 0:
                accT[r, q, b] = psum.tile([P, W], F32, name="accT", tag="acc")
            nc.tensor.matmul_mx(
                out=accT[r, q, b][:],
                lhsT=codes[r, g][:, b * P : (b + 1) * P].bitcast(E4M3X4),
                lhsT_scale=scales[r, g][:, b * P : (b + 1) * P],
                rhs=hw[g][q // 2][:, 2 * (q % 2) * W : 2 * (q % 2 + 1) * W].bitcast(E2M1X4),
                rhs_scale=hs[g][:, q * W : (q + 1) * W],
                start=(g == 0),
                stop=(g == GROUPS - 1),
            )

        def roundA(g):
            for q in range(2):
                for b in range(4):
                    productT("A", q, b, g)

        def roundT(r, q, b):
            for g in range(GROUPS):
                productT(r, q, b, g)

        def gainT(r, q, b):
            gained[r, q, b] = stage.tile([P, W], F32, name="gained", bufs=12)
            c = VT + COLS[r][0] // P + b
            if EVAC_V[f"{r}{q}{b}"]:
                nc.vector.tensor_scalar(out=gained[r, q, b][:], in0=accT[r, q, b][:], scalar1=cols[:, c : c + 1], scalar2=None, op0=MULT)
            else:
                nc.scalar.activation(out=gained[r, q, b][:], in_=accT[r, q, b][:], func=COPY, scale=cols[:, c : c + 1])

        def turn(r, i):
            q, j = divmod(i, 4)
            turned[r, i] = psum.tile([P, W], F32, name="turned", tag="acc")
            for b in range(W // P):
                nc.tensor.transpose(turned[r, i][:, b * P : (b + 1) * P], gained[r, q, b][:, j * P : (j + 1) * P], identf[:])

        def decayT(r, i):
            c0, width = COLS[r]
            o = stage.tile([P, W], F32, name="resB", bufs=6)
            nc.vector.scalar_tensor_tensor(
                out=o[:], in0=et[i // 2][:, i % 2, c0 : c0 + W], scalar=cols[:, i : i + 1], in1=turned[r, i][:], op0=MULT, op1=ADD
            )
            nc.sync.dma_start(out=out[i * P : (i + 1) * P, c0 : c0 + W], in_=o[:])

        load("G0")
        load("S0")
        load("G1")
        load("S1")
        load("Q0")
        load("R0")
        load("G3")
        load("S2")
        load("H0")
        load("S3")
        load("G2")
        load("H1")
        load("Q1")
        load("J2")
        load("H2")
        load("Q2")
        load("J0")
        load("H3")
        load("Q3")
        load("J3")
        load("J1")
        load("E2")
        load("E1")
        load("E5")
        load("E0")
        load("E3")
        load("E7")
        load("E6")
        load("E4")
        widen("A", 1)
        widen("A", 0)
        interleave("A", 0)
        turn_rows()
        quantize("A", 0)
        interleave("A", 1)
        widen("A", 3)
        roundA(0)
        widen("A", 2)
        quantize("A", 1)
        roundA(1)
        interleave("A", 2)
        quantize("A", 2)
        roundA(2)
        interleave("A", 3)
        quantize("A", 3)
        roundA(3)
        roundT("A", 2, 1)
        widen("B", 0)
        widen("B", 1)
        gainT("A", 1, 0)
        gainT("A", 0, 3)
        roundT("A", 2, 2)
        roundT("A", 2, 0)
        gainT("A", 1, 3)
        interleave("B", 0)
        roundT("A", 3, 0)
        widen("B", 3)
        gainT("A", 0, 0)
        gainT("A", 0, 2)
        gainT("A", 1, 2)
        widen("B", 2)
        roundT("A", 3, 2)
        gainT("A", 2, 1)
        quantize("B", 0)
        interleave("B", 1)
        gainT("A", 0, 1)
        turn("A", 0)
        gainT("A", 2, 2)
        gainT("A", 1, 1)
        roundT("A", 2, 3)
        turn("A", 2)
        gainT("A", 3, 2)
        decayT("A", 0)
        spread_gamma()
        quantize("B", 1)
        turn("A", 1)
        turn("A", 3)
        turn("A", 6)
        gainT("A", 2, 0)
        decayT("A", 2)
        turn("A", 5)
        roundT("A", 3, 3)
        decayT("A", 3)
        product(3, 0)
        product(0, 0)
        interleave("B", 2)
        roundT("A", 3, 1)
        product(2, 0)
        gainT("A", 3, 0)
        product(1, 0)
        gainT("A", 2, 3)
        gainT("A", 3, 3)
        product(1, 1)
        turn("A", 4)
        turn("A", 7)
        turn("A", 9)
        decayT("A", 5)
        turn("A", 11)
        decayT("A", 6)
        product(3, 1)
        quantize("B", 2)
        product(1, 2)
        decayT("A", 1)
        product(0, 1)
        product(3, 2)
        product(0, 2)
        product(2, 1)
        gainT("A", 3, 1)
        interleave("B", 3)
        product(2, 2)
        turn("A", 8)
        decayT("A", 4)
        decayT("A", 9)
        decayT("A", 7)
        turn("A", 10)
        turn("A", 12)
        quantize("B", 3)
        turn("A", 15)
        product(1, 3)
        decayT("A", 11)
        decayT("A", 8)
        product(3, 3)
        product(0, 3)
        product(2, 3)
        rows_of(6)
        turn("A", 14)
        turn("A", 13)
        rows_of(5)
        decayT("A", 10)
        roundT("B", 3, 1)
        decayT("A", 12)
        rows_of(9)
        gain(3)
        gainT("B", 3, 1)
        gain(2)
        rows_of(4)
        decayT("A", 15)
        roundT("B", 3, 2)
        gain(0)
        decay(2)
        gain(1)
        decay(0)
        decay(1)
        rows_of(7)
        gain(5)
        gainT("B", 3, 2)
        roundT("B", 3, 0)
        decayT("A", 13)
        decayT("A", 14)
        decay(5)
        gainT("B", 3, 0)
        roundT("B", 3, 3)
        gain(9)
        gain(6)
        rows_of(10)
        gainT("B", 3, 3)
        decay(3)
        decay(6)
        decay(9)
        turn("B", 13)
        turn("B", 12)
        gain(7)
        rows_of(11)
        gain(4)
        decay(7)
        turn("B", 15)
        decay(4)
        gain(10)
        decayT("B", 13)
        rows_of(8)
        decayT("B", 12)
        decay(10)
        gain(11)
        decayT("B", 15)
        decay(11)
        turn("B", 14)
        gain(8)
        decayT("B", 14)
        decay(8)
